import numpy as np
import ml_dtypes


def mxq(x, axis, fmt="e4m3"):
    dtype, down = {"e4m3": (ml_dtypes.float8_e4m3fn, 7), "e5m2": (ml_dtypes.float8_e5m2, 14)}[fmt]
    v = np.moveaxis(np.asarray(x, np.float32).astype(ml_dtypes.bfloat16).astype(np.float64), axis, -1)
    blocks = v.reshape(v.shape[:-1] + (-1, 32))
    amax = np.abs(blocks).max(-1, keepdims=True)
    byte = np.maximum(np.where(amax > 0, np.frexp(amax)[1] - 1 + 127, 0) - down, 1)
    scale = np.exp2(byte - 127.0)
    codes = (blocks / scale).astype(np.float32).astype(dtype).astype(np.float64)
    return np.moveaxis((codes * scale).reshape(v.shape), -1, axis)


WIDE = False


def mx_kscale(k):
    if not WIDE:
        return np.ones(k)
    levels = np.array([30, -30])
    if k % 512:
        return np.exp2(np.random.permutation(np.resize(levels, k // 32))).repeat(32)
    a = np.empty((k // 512, 16))
    for p in range(k // 512):
        a[p, :8] = np.random.permutation(np.resize(levels, 8))
        for g in range(8):
            far = levels[np.abs(levels - a[p, g]) >= 10]
            a[p, g + 8] = far[np.random.randint(len(far))]
    return np.exp2(a.ravel()).repeat(32)


def f64(x):
    return np.asarray(x).astype(np.float64)


E2M1 = np.array([0.0, 0.5, 1.0, 1.5, 2.0, 3.0, 4.0, 6.0, -0.0, -0.5, -1.0, -1.5, -2.0, -3.0, -4.0, -6.0])


def pack_weight(w, fmt):
    k, n = w.shape
    w = f64(np.asarray(w, np.float32).astype(ml_dtypes.bfloat16)).reshape(k // 32, 32, n)
    amax = np.abs(w).max(1)
    if fmt == "e4m3":
        byte = np.frexp(amax)[1] - 1 + 127 - 7
    else:
        mant, ex = np.frexp(amax / 6.0)
        byte = np.where(mant > 0.5, ex, ex - 1) + 127
    byte = np.clip(np.where(amax > 0, byte, 1), 1, 254)
    scaled = (w * np.exp2(127.0 - byte)[:, None, :]).reshape(k, n).astype(np.float32)
    by_word = np.ascontiguousarray(scaled.reshape(k // 512, 128, 4, n).transpose(0, 1, 3, 2))
    if fmt == "e4m3":
        words = by_word.astype(ml_dtypes.float8_e4m3fn).view(np.uint8)
    else:
        c = by_word.astype(ml_dtypes.float4_e2m1fn).view(np.uint8) & 0xF
        words = (c[..., 0::2] | (c[..., 1::2] << 4)).reshape(k // 512, 128, 2 * n)
    return np.ascontiguousarray(words), np.ascontiguousarray(byte.astype(np.uint8).reshape(k // 512, 16, n))


def unpack_weight(words, scales, fmt):
    g, _, n = scales.shape
    words = np.ascontiguousarray(words).reshape(g, 128, n, -1)
    if fmt == "e4m3":
        vals = words.view(ml_dtypes.float8_e4m3fn).astype(np.float64)
    else:
        nib = np.empty((g, 128, n, 4), np.uint8)
        nib[..., 0::2] = words & 0xF
        nib[..., 1::2] = words >> 4
        vals = E2M1[nib]
    vals = vals * np.repeat(np.exp2(scales.astype(np.float64) - 127.0), 8, axis=1)[..., None]
    return vals.transpose(0, 1, 3, 2).reshape(g * 512, n)


O, K, M, T = 1024, 2560, 1536, 512


def setup_inputs():
    n = np.random.standard_normal
    s = mx_kscale(K)[:, None]
    dy = np.exp(0.5 * n((1, T))) * n((K, T))
    w = n((K, M)) / np.sqrt(K) / s
    p_w8 = pack_weight(w[:O], "e4m3")
    p_w4 = pack_weight(w[O:], "e2m1")
    return {
        "dy": (dy * s).astype(np.float32),
        "w8_words": p_w8[0],
        "w8_scales": p_w8[1],
        "w4_words": p_w4[0],
        "w4_scales": p_w4[1],
        "g": (n((1536, 512))).astype(np.float32),
    }


def reference(dy, w8_words, w8_scales, w4_words, w4_scales, g):
    dy_ = mxq(f64(dy), 0, "e5m2")
    w8_ = unpack_weight(w8_words, w8_scales, "e4m3")
    w4_ = unpack_weight(w4_words, w4_scales, "e2m1")
    y = w8_.T @ dy_[:O] + w4_.T @ dy_[O:]
    return f64(g) * y

@@ -1,0 +1,128 @@
+from contextlib import ExitStack
+
+import concourse.mybir as mybir
+
+F32 = mybir.dt.float32
+BF16 = mybir.dt.bfloat16
+U32 = mybir.dt.uint32
+I32 = mybir.dt.int32
+U8 = mybir.dt.uint8
+E5M2X4 = mybir.dt.float8_e5m2_x4
+E4M3X4 = mybir.dt.float8_e4m3fn_x4
+E2M1X4 = mybir.dt.float4_e2m1fn_x4
+MULT = mybir.AluOpType.mult
+
+O, K, M, T = 1024, 2560, 1536, 512
+FLOPS = 2 * K * M * T
+
+P = 128
+PACK = 4
+K_PASS = P * PACK
+PASSES8 = O // K_PASS
+PASSES4 = (K - O) // K_PASS
+PASSES = PASSES8 + PASSES4
+D_TILE = 128
+D_TILES = M // D_TILE
+BANKS = 8
+VECTOR_COLS = 352
+
+
+def tile_mix_dyq_fm_mul_kernel(tc, dy, w8_words, w8_scales, w4_words, w4_scales, g, out):
+    nc = tc.nc
+    with ExitStack() as ctx:
+        keep = ctx.enter_context(tc.tile_pool(name="keep", bufs=1))
+        psum = ctx.enter_context(tc.psum_pool(name="psum", bufs=1))
+        ctx.enter_context(tc.manual_schedule())
+
+        raw = [keep.tile([P, PACK, T], F32, name=f"raw{a}", align_bytes=64) for a in range(PASSES)]
+        grouped = [keep.tile([P, T, PACK], BF16, name=f"grouped{a}", align_bytes=64) for a in range(PASSES)]
+        codes = [keep.tile([P, T], U32, name=f"codes{a}", align_bytes=64) for a in range(PASSES)]
+        planes = [keep.tile([P, T], U8, name=f"planes{a}", align_bytes=64) for a in range(PASSES)]
+        w8 = [keep.tile([P, M], U32, name=f"w8_{a}", align_bytes=64) for a in range(PASSES8)]
+        w4 = [keep.tile([P, 2 * M], U8, name=f"w4_{a}", align_bytes=64) for a in range(PASSES4)]
+        s8 = keep.tile([P, PASSES8, M], U8, name="s8", align_bytes=64)
+        s4 = keep.tile([P, PASSES4, M], U8, name="s4", align_bytes=64)
+        gates = [keep.tile([D_TILE, T], F32, name=f"gate{i}", align_bytes=64) for i in range(D_TILES)]
+        results = [keep.tile([D_TILE, T], F32, name=f"result{i}", align_bytes=64) for i in range(D_TILES)]
+
+
+        def load_dy(a):
+            nc.sync.dma_start(out=raw[a][:], in_=dy[a * K_PASS : (a + 1) * K_PASS, :].rearrange("(p j) t -> p j t", j=PACK))
+
+        def load_w8(a):
+            nc.sync.dma_start(out=w8[a][:].bitcast(I32), in_=w8_words[a].rearrange("p n t -> p (n t)").bitcast(I32))
+
+        def load_w4(a):
+            nc.sync.dma_start(out=w4[a][:].bitcast(I32), in_=w4_words[a].bitcast(I32))
+
+        def load_scales(engine, tile, scales):
+            source = scales.bitcast(I32).rearrange("a (q r) n -> r q a n", r=4)
+            target = tile[:].bitcast(I32)
+            for r in range(4):
+                engine.dma_start(out=target[r:P:32, :, :], in_=source[r])
+
+        def group(a):
+            source = raw[a][:].rearrange("p j (c i) -> p c j i", i=4)
+            target = grouped[a][:].rearrange("p (c i) j -> p c j i", i=4)
+            cut = VECTOR_COLS // 4
+            nc.vector.tensor_copy(out=target[:, :cut], in_=source[:, :cut])
+            nc.scalar.copy(out=target[:, cut:], in_=source[:, cut:])
+
+        def quantize(a):
+            nc.vector.quantize_mx(
+                out=codes[a][:].bitcast(E5M2X4), scales=planes[a][:], in_=grouped[a][:].rearrange("p t j -> p (t j)")
+            )
+
+        def multiply(acc, i, a):
+            d0 = i * D_TILE
+            if a < PASSES8:
+                weight = w8[a][:, d0 : d0 + D_TILE].bitcast(E4M3X4)
+                weight_scale = s8[:, a, d0 : d0 + D_TILE]
+            else:
+                b = a - PASSES8
+                weight = w4[b][:, 2 * d0 : 2 * (d0 + D_TILE)].bitcast(E2M1X4)
+                weight_scale = s4[:, b, d0 : d0 + D_TILE]
+            nc.tensor.matmul_mx(
+                out=acc[:],
+                lhsT=weight,
+                lhsT_scale=weight_scale,
+                rhs=codes[a][:].bitcast(E5M2X4),
+                rhs_scale=planes[a][:],
+                start=(a == 0),
+                stop=(a == PASSES - 1),
+            )
+
+        def bank(i):
+            return psum.tile([D_TILE, T], F32, name=f"bank{i % BANKS}")
+
+        def finish(acc, i):
+            nc.vector.tensor_tensor(out=results[i][:], in0=acc[:], in1=gates[i][:], op=MULT)
+            nc.sync.dma_start(out=out[i * D_TILE : (i + 1) * D_TILE, :], in_=results[i][:])
+
+        nc.vector.memset(s8[:].bitcast(I32), 0)
+        nc.vector.memset(s4[:].bitcast(I32), 0)
+        load_dy(0)
+        load_scales(nc.gpsimd, s8, w8_scales)
+        load_w8(0)
+        load_dy(1)
+        load_w8(1)
+        load_scales(nc.gpsimd, s4, w4_scales)
+        for b in range(PASSES4):
+            load_w4(b)
+            load_dy(PASSES8 + b)
+        for i in range(D_TILES):
+            nc.sync.dma_start(out=gates[i][:], in_=g[i * D_TILE : (i + 1) * D_TILE, :])
+
+        first = [bank(i) for i in range(BANKS)]
+        for a in range(PASSES):
+            group(a)
+            quantize(a)
+            for i in range(BANKS):
+                multiply(first[i], i, a)
+        for i in range(BANKS):
+            finish(first[i], i)
+        for i in range(BANKS, D_TILES):
+            acc = bank(i)
+            for a in range(PASSES):
+                multiply(acc, i, a)
+            finish(acc, i)

@@ -21,9 +21,10 @@ K_PASS = P * PACK
 PASSES8 = O // K_PASS
 PASSES4 = (K - O) // K_PASS
 PASSES = PASSES8 + PASSES4
-D_TILE = 128
-D_TILES = M // D_TILE
-BANKS = 8
+ROWS = 4
+BLOCK = P * ROWS
+BLOCKS = M // BLOCK
+SORTED = 2
 VECTOR_COLS = 352
 
 
@@ -38,22 +39,33 @@ def tile_mix_dyq_fm_mul_kernel(tc, dy, w8_words, w8_scales, w4_words, w4_scales,
         grouped = [keep.tile([P, T, PACK], BF16, name=f"grouped{a}", align_bytes=64) for a in range(PASSES)]
         codes = [keep.tile([P, T], U32, name=f"codes{a}", align_bytes=64) for a in range(PASSES)]
         planes = [keep.tile([P, T], U8, name=f"planes{a}", align_bytes=64) for a in range(PASSES)]
-        w8 = [keep.tile([P, M], U32, name=f"w8_{a}", align_bytes=64) for a in range(PASSES8)]
-        w4 = [keep.tile([P, 2 * M], U8, name=f"w4_{a}", align_bytes=64) for a in range(PASSES4)]
-        s8 = keep.tile([P, PASSES8, M], U8, name="s8", align_bytes=64)
-        s4 = keep.tile([P, PASSES4, M], U8, name="s4", align_bytes=64)
-        gates = [keep.tile([D_TILE, T], F32, name=f"gate{i}", align_bytes=64) for i in range(D_TILES)]
-        results = [keep.tile([D_TILE, T], F32, name=f"result{i}", align_bytes=64) for i in range(D_TILES)]
-
+        w8_in = [keep.tile([P, SORTED * BLOCK], I32, name=f"w8_in{a}", align_bytes=64) for a in range(PASSES8)]
+        w4_in = [keep.tile([P, 2 * SORTED * BLOCK], U8, name=f"w4_in{a}", align_bytes=64) for a in range(PASSES4)]
+        w8_last = keep.tile([P, PASSES8, BLOCK], I32, name="w8_last", align_bytes=64)
+        w4_last = keep.tile([P, PASSES4, 2 * BLOCK], U8, name="w4_last", align_bytes=64)
+        s8_in = keep.tile([P, PASSES8, M], U8, name="s8_in", align_bytes=64)
+        s4_in = keep.tile([P, PASSES4, M], U8, name="s4_in", align_bytes=64)
+        w8 = [keep.tile([P, SORTED * BLOCK], I32, name=f"w8_{a}", align_bytes=64) for a in range(PASSES8)]
+        w4 = [keep.tile([P, 2 * SORTED * BLOCK], U8, name=f"w4_{a}", align_bytes=64) for a in range(PASSES4)]
+        s8 = [keep.tile([P, SORTED * BLOCK], U8, name=f"s8_{a}", align_bytes=64) for a in range(PASSES8)]
+        s4 = [keep.tile([P, SORTED * BLOCK], U8, name=f"s4_{a}", align_bytes=64) for a in range(PASSES4)]
+        gates = [keep.tile([P, ROWS, T], F32, name=f"gate{c}", align_bytes=64) for c in range(BLOCKS)]
+        results = [keep.tile([P, ROWS, T], F32, name=f"result{c}", align_bytes=64) for c in range(BLOCKS)]
 
         def load_dy(a):
             nc.sync.dma_start(out=raw[a][:], in_=dy[a * K_PASS : (a + 1) * K_PASS, :].rearrange("(p j) t -> p j t", j=PACK))
 
         def load_w8(a):
-            nc.sync.dma_start(out=w8[a][:].bitcast(I32), in_=w8_words[a].rearrange("p n t -> p (n t)").bitcast(I32))
+            nc.sync.dma_start(out=w8_in[a][:], in_=w8_words.rearrange("a p n t -> a p (n t)").bitcast(I32)[a][:, : SORTED * BLOCK])
 
         def load_w4(a):
-            nc.sync.dma_start(out=w4[a][:].bitcast(I32), in_=w4_words[a].bitcast(I32))
+            nc.sync.dma_start(out=w4_in[a][:].bitcast(I32), in_=w4_words.bitcast(I32)[a][:, : SORTED * BLOCK // 2])
+
+        def load_last_block():
+            w8_view = w8_words.rearrange("a p n t -> p a (n t)").bitcast(I32)
+            w4_view = w4_words.rearrange("a p n -> p a n").bitcast(I32)
+            nc.sync.dma_start(out=w8_last[:], in_=w8_view[:, :, SORTED * BLOCK :])
+            nc.sync.dma_start(out=w4_last[:].bitcast(I32), in_=w4_view[:, :, SORTED * BLOCK // 2 :])
 
         def load_scales(engine, tile, scales):
             source = scales.bitcast(I32).rearrange("a (q r) n -> r q a n", r=4)
@@ -61,11 +73,23 @@ def tile_mix_dyq_fm_mul_kernel(tc, dy, w8_words, w8_scales, w4_words, w4_scales,
             for r in range(4):
                 engine.dma_start(out=target[r:P:32, :, :], in_=source[r])
 
-        def group(a):
+        def sort_columns(target, source, width, c0, c1):
+            for c in range(c0, c1):
+                lo, hi = c * BLOCK * width, (c + 1) * BLOCK * width
+                if width == 1:
+                    result = target[:, lo:hi].rearrange("p (j m) -> p j m", j=ROWS)
+                    source_view = source[:, lo:hi].rearrange("p (m j) -> p j m", j=ROWS)
+                else:
+                    result = target[:, lo:hi].rearrange("p (j m b) -> p j m b", j=ROWS, b=width)
+                    source_view = source[:, lo:hi].rearrange("p (m j b) -> p j m b", j=ROWS, b=width)
+                nc.vector.tensor_copy(out=result, in_=source_view)
+
+        def group(a, vector_cols):
             source = raw[a][:].rearrange("p j (c i) -> p c j i", i=4)
             target = grouped[a][:].rearrange("p (c i) j -> p c j i", i=4)
-            cut = VECTOR_COLS // 4
-            nc.vector.tensor_copy(out=target[:, :cut], in_=source[:, :cut])
+            cut = vector_cols // 4
+            if cut:
+                nc.vector.tensor_copy(out=target[:, :cut], in_=source[:, :cut])
             nc.scalar.copy(out=target[:, cut:], in_=source[:, cut:])
 
         def quantize(a):
@@ -73,15 +97,17 @@ def tile_mix_dyq_fm_mul_kernel(tc, dy, w8_words, w8_scales, w4_words, w4_scales,
                 out=codes[a][:].bitcast(E5M2X4), scales=planes[a][:], in_=grouped[a][:].rearrange("p t j -> p (t j)")
             )
 
-        def multiply(acc, i, a):
-            d0 = i * D_TILE
+        def multiply(acc, c, j, a):
+            d0 = c * BLOCK + j * P
+            b = a - PASSES8
             if a < PASSES8:
-                weight = w8[a][:, d0 : d0 + D_TILE].bitcast(E4M3X4)
-                weight_scale = s8[:, a, d0 : d0 + D_TILE]
+                words = w8[a][:, d0 : d0 + P] if c < SORTED else w8_last[:, a, j * P : (j + 1) * P]
+                weight = words.bitcast(E4M3X4)
+                weight_scale = (s8[a][:] if c < SORTED else s8_in[:, a, :])[:, d0 : d0 + P]
             else:
-                b = a - PASSES8
-                weight = w4[b][:, 2 * d0 : 2 * (d0 + D_TILE)].bitcast(E2M1X4)
-                weight_scale = s4[:, b, d0 : d0 + D_TILE]
+                words = w4[b][:, 2 * d0 : 2 * (d0 + P)] if c < SORTED else w4_last[:, b, 2 * j * P : 2 * (j + 1) * P]
+                weight = words.bitcast(E2M1X4)
+                weight_scale = (s4[b][:] if c < SORTED else s4_in[:, b, :])[:, d0 : d0 + P]
             nc.tensor.matmul_mx(
                 out=acc[:],
                 lhsT=weight,
@@ -93,36 +119,60 @@ def tile_mix_dyq_fm_mul_kernel(tc, dy, w8_words, w8_scales, w4_words, w4_scales,
             )
 
         def bank(i):
-            return psum.tile([D_TILE, T], F32, name=f"bank{i % BANKS}")
+            return psum.tile([P, T], F32, name=f"bank{i % 8}")
 
-        def finish(acc, i):
-            nc.vector.tensor_tensor(out=results[i][:], in0=acc[:], in1=gates[i][:], op=MULT)
-            nc.sync.dma_start(out=out[i * D_TILE : (i + 1) * D_TILE, :], in_=results[i][:])
+        def finish(acc, c, j):
+            nc.vector.tensor_tensor(out=results[c][:, j, :], in0=acc[:], in1=gates[c][:, j, :], op=MULT)
 
-        nc.vector.memset(s8[:].bitcast(I32), 0)
-        nc.vector.memset(s4[:].bitcast(I32), 0)
+        def rows(tensor, c):
+            block = tensor[c * BLOCK : (c + 1) * BLOCK, :]
+            return block.rearrange("(p j) t -> p j t", j=ROWS) if c < SORTED else block.rearrange("(j p) t -> p j t", j=ROWS)
+
+        def load_g(c, j0, j1):
+            nc.sync.dma_start(out=gates[c][:, j0:j1, :], in_=rows(g, c)[:, j0:j1, :])
+
+        def store(c, j0, j1):
+            nc.sync.dma_start(out=rows(out, c)[:, j0:j1, :], in_=results[c][:, j0:j1, :])
+
+        nc.vector.memset(s8_in[:].bitcast(I32), 0)
+        nc.vector.memset(s4_in[:].bitcast(I32), 0)
         load_dy(0)
-        load_scales(nc.gpsimd, s8, w8_scales)
+        load_scales(nc.sync, s8_in, w8_scales)
         load_w8(0)
         load_dy(1)
+        load_scales(nc.sync, s4_in, w4_scales)
         load_w8(1)
-        load_scales(nc.gpsimd, s4, w4_scales)
         for b in range(PASSES4):
             load_w4(b)
             load_dy(PASSES8 + b)
-        for i in range(D_TILES):
-            nc.sync.dma_start(out=gates[i][:], in_=g[i * D_TILE : (i + 1) * D_TILE, :])
+        load_last_block()
+        for c in range(SORTED):
+            load_g(c, 0, ROWS)
+        for j in range(ROWS):
+            load_g(SORTED, j, j + 1)
 
-        first = [bank(i) for i in range(BANKS)]
+        tiles = [(c, j) for c in range(BLOCKS) for j in range(ROWS)]
+        first = [bank(i) for i in range(8)]
+
         for a in range(PASSES):
-            group(a)
+            if a < PASSES8:
+                sort_columns(s8[a], s8_in[:, a, :], 1, 0, SORTED)
+                sort_columns(w8[a], w8_in[a], 1, 0, SORTED)
+            else:
+                b = a - PASSES8
+                sort_columns(s4[b], s4_in[:, b, :], 1, 0, SORTED)
+                sort_columns(w4[b], w4_in[b], 2, 0, SORTED)
+            group(a, VECTOR_COLS if a == PASSES - 1 else 0)
             quantize(a)
-            for i in range(BANKS):
-                multiply(first[i], i, a)
-        for i in range(BANKS):
-            finish(first[i], i)
-        for i in range(BANKS, D_TILES):
-            acc = bank(i)
+            for i in range(8):
+                multiply(first[i], *tiles[i], a)
+        for i in range(8):
+            finish(first[i], *tiles[i])
+            if i % 2:
+                store(tiles[i][0], tiles[i][1] - 1, tiles[i][1] + 1)
+        for j in range(ROWS):
+            acc = bank(j)
             for a in range(PASSES):
-                multiply(acc, i, a)
-            finish(acc, i)
+                multiply(acc, SORTED, j, a)
+            finish(acc, SORTED, j)
+            store(SORTED, j, j + 1)

from contextlib import ExitStack

import concourse.mybir as mybir

F32 = mybir.dt.float32
BF16 = mybir.dt.bfloat16
U32 = mybir.dt.uint32
I32 = mybir.dt.int32
U8 = mybir.dt.uint8
E5M2X4 = mybir.dt.float8_e5m2_x4
E4M3X4 = mybir.dt.float8_e4m3fn_x4
E2M1X4 = mybir.dt.float4_e2m1fn_x4
MULT = mybir.AluOpType.mult

O, K, M, T = 1024, 2560, 1536, 512
FLOPS = 2 * K * M * T

P = 128
PACK = 4
K_PASS = P * PACK
PASSES8 = O // K_PASS
PASSES4 = (K - O) // K_PASS
PASSES = PASSES8 + PASSES4
ROWS = 4
BLOCK = P * ROWS
BLOCKS = M // BLOCK
SORTED = 2
VECTOR_COLS = 352


def tile_mix_dyq_fm_mul_kernel(tc, dy, w8_words, w8_scales, w4_words, w4_scales, g, out):
    nc = tc.nc
    with ExitStack() as ctx:
        keep = ctx.enter_context(tc.tile_pool(name="keep", bufs=1))
        psum = ctx.enter_context(tc.psum_pool(name="psum", bufs=1))
        ctx.enter_context(tc.manual_schedule())

        raw = [keep.tile([P, PACK, T], F32, name=f"raw{a}", align_bytes=64) for a in range(PASSES)]
        grouped = [keep.tile([P, T, PACK], BF16, name=f"grouped{a}", align_bytes=64) for a in range(PASSES)]
        codes = [keep.tile([P, T], U32, name=f"codes{a}", align_bytes=64) for a in range(PASSES)]
        planes = [keep.tile([P, T], U8, name=f"planes{a}", align_bytes=64) for a in range(PASSES)]
        w8_in = [keep.tile([P, SORTED * BLOCK], I32, name=f"w8_in{a}", align_bytes=64) for a in range(PASSES8)]
        w4_in = [keep.tile([P, 2 * SORTED * BLOCK], U8, name=f"w4_in{a}", align_bytes=64) for a in range(PASSES4)]
        w8_last = keep.tile([P, PASSES8, BLOCK], I32, name="w8_last", align_bytes=64)
        w4_last = keep.tile([P, PASSES4, 2 * BLOCK], U8, name="w4_last", align_bytes=64)
        s8_in = keep.tile([P, PASSES8, M], U8, name="s8_in", align_bytes=64)
        s4_in = keep.tile([P, PASSES4, M], U8, name="s4_in", align_bytes=64)
        w8 = [keep.tile([P, SORTED * BLOCK], I32, name=f"w8_{a}", align_bytes=64) for a in range(PASSES8)]
        w4 = [keep.tile([P, 2 * SORTED * BLOCK], U8, name=f"w4_{a}", align_bytes=64) for a in range(PASSES4)]
        s8 = [keep.tile([P, SORTED * BLOCK], U8, name=f"s8_{a}", align_bytes=64) for a in range(PASSES8)]
        s4 = [keep.tile([P, SORTED * BLOCK], U8, name=f"s4_{a}", align_bytes=64) for a in range(PASSES4)]
        gates = [keep.tile([P, ROWS, T], F32, name=f"gate{c}", align_bytes=64) for c in range(BLOCKS)]
        results = [keep.tile([P, ROWS, T], F32, name=f"result{c}", align_bytes=64) for c in range(BLOCKS)]

        def load_dy(a):
            nc.sync.dma_start(out=raw[a][:], in_=dy[a * K_PASS : (a + 1) * K_PASS, :].rearrange("(p j) t -> p j t", j=PACK))

        def load_w8(a):
            nc.sync.dma_start(out=w8_in[a][:], in_=w8_words.rearrange("a p n t -> a p (n t)").bitcast(I32)[a][:, : SORTED * BLOCK])

        def load_w4(a):
            nc.sync.dma_start(out=w4_in[a][:].bitcast(I32), in_=w4_words.bitcast(I32)[a][:, : SORTED * BLOCK // 2])

        def load_last_block():
            w8_view = w8_words.rearrange("a p n t -> p a (n t)").bitcast(I32)
            w4_view = w4_words.rearrange("a p n -> p a n").bitcast(I32)
            nc.sync.dma_start(out=w8_last[:], in_=w8_view[:, :, SORTED * BLOCK :])
            nc.sync.dma_start(out=w4_last[:].bitcast(I32), in_=w4_view[:, :, SORTED * BLOCK // 2 :])

        def load_scales(engine, tile, scales):
            source = scales.bitcast(I32).rearrange("a (q r) n -> r q a n", r=4)
            target = tile[:].bitcast(I32)
            for r in range(4):
                engine.dma_start(out=target[r:P:32, :, :], in_=source[r])

        def sort_columns(target, source, width, c0, c1):
            for c in range(c0, c1):
                lo, hi = c * BLOCK * width, (c + 1) * BLOCK * width
                if width == 1:
                    result = target[:, lo:hi].rearrange("p (j m) -> p j m", j=ROWS)
                    source_view = source[:, lo:hi].rearrange("p (m j) -> p j m", j=ROWS)
                else:
                    result = target[:, lo:hi].rearrange("p (j m b) -> p j m b", j=ROWS, b=width)
                    source_view = source[:, lo:hi].rearrange("p (m j b) -> p j m b", j=ROWS, b=width)
                nc.vector.tensor_copy(out=result, in_=source_view)

        def group(a, vector_cols):
            source = raw[a][:].rearrange("p j (c i) -> p c j i", i=4)
            target = grouped[a][:].rearrange("p (c i) j -> p c j i", i=4)
            cut = vector_cols // 4
            if cut:
                nc.vector.tensor_copy(out=target[:, :cut], in_=source[:, :cut])
            nc.scalar.copy(out=target[:, cut:], in_=source[:, cut:])

        def quantize(a):
            nc.vector.quantize_mx(
                out=codes[a][:].bitcast(E5M2X4), scales=planes[a][:], in_=grouped[a][:].rearrange("p t j -> p (t j)")
            )

        def multiply(acc, c, j, a):
            d0 = c * BLOCK + j * P
            b = a - PASSES8
            if a < PASSES8:
                words = w8[a][:, d0 : d0 + P] if c < SORTED else w8_last[:, a, j * P : (j + 1) * P]
                weight = words.bitcast(E4M3X4)
                weight_scale = (s8[a][:] if c < SORTED else s8_in[:, a, :])[:, d0 : d0 + P]
            else:
                words = w4[b][:, 2 * d0 : 2 * (d0 + P)] if c < SORTED else w4_last[:, b, 2 * j * P : 2 * (j + 1) * P]
                weight = words.bitcast(E2M1X4)
                weight_scale = (s4[b][:] if c < SORTED else s4_in[:, b, :])[:, d0 : d0 + P]
            nc.tensor.matmul_mx(
                out=acc[:],
                lhsT=weight,
                lhsT_scale=weight_scale,
                rhs=codes[a][:].bitcast(E5M2X4),
                rhs_scale=planes[a][:],
                start=(a == 0),
                stop=(a == PASSES - 1),
            )

        def bank(i):
            return psum.tile([P, T], F32, name=f"bank{i % 8}")

        def finish(acc, c, j):
            nc.vector.tensor_tensor(out=results[c][:, j, :], in0=acc[:], in1=gates[c][:, j, :], op=MULT)

        def rows(tensor, c):
            block = tensor[c * BLOCK : (c + 1) * BLOCK, :]
            return block.rearrange("(p j) t -> p j t", j=ROWS) if c < SORTED else block.rearrange("(j p) t -> p j t", j=ROWS)

        def load_g(c, j0, j1):
            nc.sync.dma_start(out=gates[c][:, j0:j1, :], in_=rows(g, c)[:, j0:j1, :])

        def store(c, j0, j1):
            nc.sync.dma_start(out=rows(out, c)[:, j0:j1, :], in_=results[c][:, j0:j1, :])

        nc.vector.memset(s8_in[:].bitcast(I32), 0)
        nc.vector.memset(s4_in[:].bitcast(I32), 0)
        load_dy(0)
        load_scales(nc.sync, s8_in, w8_scales)
        load_w8(0)
        load_dy(1)
        load_scales(nc.sync, s4_in, w4_scales)
        load_w8(1)
        for b in range(PASSES4):
            load_w4(b)
            load_dy(PASSES8 + b)
        load_last_block()
        for c in range(SORTED):
            load_g(c, 0, ROWS)
        for j in range(ROWS):
            load_g(SORTED, j, j + 1)

        tiles = [(c, j) for c in range(BLOCKS) for j in range(ROWS)]
        first = [bank(i) for i in range(8)]

        for a in range(PASSES):
            if a < PASSES8:
                sort_columns(s8[a], s8_in[:, a, :], 1, 0, SORTED)
                sort_columns(w8[a], w8_in[a], 1, 0, SORTED)
            else:
                b = a - PASSES8
                sort_columns(s4[b], s4_in[:, b, :], 1, 0, SORTED)
                sort_columns(w4[b], w4_in[b], 2, 0, SORTED)
            group(a, VECTOR_COLS if a == PASSES - 1 else 0)
            quantize(a)
            for i in range(8):
                multiply(first[i], *tiles[i], a)
        for i in range(8):
            finish(first[i], *tiles[i])
            if i % 2:
                store(tiles[i][0], tiles[i][1] - 1, tiles[i][1] + 1)
        for j in range(ROWS):
            acc = bank(j)
            for a in range(PASSES):
                multiply(acc, SORTED, j, a)
            finish(acc, SORTED, j)
            store(SORTED, j, j + 1)
